import numpy as np
import ml_dtypes


def mxq(x, axis, fmt="e4m3"):
    dtype, down = {"e4m3": (ml_dtypes.float8_e4m3fn, 7), "e5m2": (ml_dtypes.float8_e5m2, 14)}[fmt]
    v = np.moveaxis(np.asarray(x, np.float32).astype(ml_dtypes.bfloat16).astype(np.float64), axis, -1)
    blocks = v.reshape(v.shape[:-1] + (-1, 32))
    amax = np.abs(blocks).max(-1, keepdims=True)
    byte = np.maximum(np.where(amax > 0, np.frexp(amax)[1] - 1 + 127, 0) - down, 1)
    scale = np.exp2(byte - 127.0)
    codes = (blocks / scale).astype(np.float32).astype(dtype).astype(np.float64)
    return np.moveaxis((codes * scale).reshape(v.shape), -1, axis)


WIDE = False


def mx_kscale(k):
    if not WIDE:
        return np.ones(k)
    levels = np.array([10, -10, 5, -5, 0])
    if k % 512:
        return np.exp2(np.random.permutation(np.resize(levels, k // 32))).repeat(32)
    a = np.empty((k // 512, 16))
    for p in range(k // 512):
        a[p, :8] = np.random.permutation(np.resize(levels, 8))
        for g in range(8):
            far = levels[np.abs(levels - a[p, g]) >= 10]
            a[p, g + 8] = far[np.random.randint(len(far))]
    return np.exp2(a.ravel()).repeat(32)


def f64(x):
    return np.asarray(x).astype(np.float64)


def striped(idx):
    return np.tile(idx.reshape(-1, 16).T, (8, 1)).astype(np.uint16)


def unstriped(offs):
    return offs[:16].T.reshape(-1).astype(np.int64)


E2M1 = np.array([0.0, 0.5, 1.0, 1.5, 2.0, 3.0, 4.0, 6.0, -0.0, -0.5, -1.0, -1.5, -2.0, -3.0, -4.0, -6.0])


def pack_weight(w, fmt):
    k, n = w.shape
    w = f64(np.asarray(w, np.float32).astype(ml_dtypes.bfloat16)).reshape(k // 32, 32, n)
    amax = np.abs(w).max(1)
    if fmt == "e4m3":
        byte = np.frexp(amax)[1] - 1 + 127 - 7
    else:
        mant, ex = np.frexp(amax / 6.0)
        byte = np.where(mant > 0.5, ex, ex - 1) + 127
    byte = np.clip(np.where(amax > 0, byte, 1), 1, 254)
    scaled = (w * np.exp2(127.0 - byte)[:, None, :]).reshape(k, n).astype(np.float32)
    by_word = np.ascontiguousarray(scaled.reshape(k // 512, 128, 4, n).transpose(0, 1, 3, 2))
    if fmt == "e4m3":
        words = by_word.astype(ml_dtypes.float8_e4m3fn).view(np.uint8)
    else:
        c = by_word.astype(ml_dtypes.float4_e2m1fn).view(np.uint8) & 0xF
        words = (c[..., 0::2] | (c[..., 1::2] << 4)).reshape(k // 512, 128, 2 * n)
    return np.ascontiguousarray(words), np.ascontiguousarray(byte.astype(np.uint8).reshape(k // 512, 16, n))


def unpack_weight(words, scales, fmt):
    g, _, n = scales.shape
    words = np.ascontiguousarray(words).reshape(g, 128, n, -1)
    if fmt == "e4m3":
        vals = words.view(ml_dtypes.float8_e4m3fn).astype(np.float64)
    else:
        nib = np.empty((g, 128, n, 4), np.uint8)
        nib[..., 0::2] = words & 0xF
        nib[..., 1::2] = words >> 4
        vals = E2M1[nib]
    vals = vals * np.repeat(np.exp2(scales.astype(np.float64) - 127.0), 8, axis=1)[..., None]
    return vals.transpose(0, 1, 3, 2).reshape(g * 512, n)


def gelu(v):
    return 0.5 * v * (1.0 + np.tanh(np.sqrt(2.0 / np.pi) * (v + 0.044715 * v**3)))


def striped8(idx):
    return np.concatenate([v.reshape(-1, 16).T for v in idx]).astype(np.uint16)


def unstriped8(offs):
    return np.stack([offs[16 * g:16 * g + 16].T.reshape(-1) for g in range(8)]).astype(np.int64)


def heads(h, wgt, idx8):
    r = np.arange(h.shape[0])
    return wgt[r // 4 % 128] * h[r[:, None], idx8[r % 512 // 64]]


def put_heads(h, wgs, idx8, t2):
    r = np.arange(h.shape[0])
    page = np.zeros((h.shape[0], t2))
    page[r[:, None], idx8[r % 512 // 64]] = wgs[r // 4 % 128] * h
    return page


K, T, S, H, T2, P, N = 1024, 4096, 1024, 1024, 2048, 1024, 384

def setup_inputs():
    n = np.random.standard_normal
    s = mx_kscale(K)[:, None]
    u = mx_kscale(H)[:, None]
    d = {}
    d["tab_words"], d["tab_scales"] = pack_weight(n((K, T)) * s, "e4m3")
    d["offs"] = striped(np.random.permutation(T)[:S])
    d["offs2"] = striped8(np.stack([np.random.permutation(T2)[:S] for _ in range(8)]))
    d["offs3"] = striped8(np.stack([np.random.permutation(T2)[:P] for _ in range(8)]))
    d["wgs"] = np.repeat(np.random.uniform(0.5, 2.0, (8, S)), 16, axis=0).astype(np.float32)
    d["wgt"] = np.repeat(np.random.uniform(0.5, 2.0, (8, P)), 16, axis=0).astype(np.float32)
    d["w1"] = (1.5 * n((K, H)) / K**0.5 / s).astype(np.float32)
    d["gain"] = (np.exp(0.3 * n(H)) * u[:, 0]).astype(np.float32)
    d["cloth"] = (n((H, P)) * u).astype(np.float32)
    d["wa_words"], d["wa_scales"] = pack_weight(n((H, N)) / H**0.5 / u, "e2m1")
    d["wb"] = (n((H, N)) / H**0.5 / u).astype(np.float32)
    d["wc"] = (1.5 * n((H, N)) / H**0.5 / u).astype(np.float32)
    d["cap"] = (0.6 + 0.4 * n(N)).astype(np.float32)
    return d

def reference(tab_words, tab_scales, offs, offs2, offs3, wgs, wgt, w1, gain, cloth, wa_words, wa_scales, wb, wc, cap):
    v = unpack_weight(tab_words, tab_scales, "e4m3")[:, unstriped(offs)]
    h = np.tanh(mxq(f64(w1), 0, "e4m3").T @ v) * f64(gain)[:, None]
    page = put_heads(h, f64(wgs), unstriped8(offs2), T2)
    x = heads(page, f64(wgt), unstriped8(offs3))
    z = mxq(x + f64(cloth), 0, "e4m3")
    wa = unpack_weight(wa_words, wa_scales, "e2m1")
    ya = wa.T @ z
    yb = mxq(f64(wb), 0, "e4m3").T @ z
    yc = mxq(f64(wc), 0, "e4m3").T @ mxq(h, 0, "e4m3")
    return np.minimum(np.maximum(ya, yb), yc + f64(cap)[:, None])

@@ -1,0 +1,311 @@
+from contextlib import ExitStack
+
+import concourse.mybir as mybir
+from concourse.masks import make_identity
+
+K, T, S, H, T2, PCOLS, N = 1024, 4096, 1024, 1024, 2048, 1024, 384
+FLOPS = 2 * K * H * S + 3 * 2 * H * N * PCOLS
+
+F32 = mybir.dt.float32
+BF16 = mybir.dt.bfloat16
+I32 = mybir.dt.int32
+U32 = mybir.dt.uint32
+U16 = mybir.dt.uint16
+U8 = mybir.dt.uint8
+FP8X4 = mybir.dt.float8_e4m3fn_x4
+FP4X4 = mybir.dt.float4_e2m1fn_x4
+ALU = mybir.AluOpType
+ACT = mybir.ActivationFunctionType
+
+P = 128
+PACK = 4
+PASS = P * PACK
+HALF = 512
+
+
+def tile_list_snooker_foul_review_kernel(tc, tab_words, tab_scales, offs, offs2, offs3, wgs, wgt, w1, gain,
+                                                   cloth, wa_words, wa_scales, wb, wc, cap, out):
+    nc = tc.nc
+    with ExitStack() as ctx:
+        lists = ctx.enter_context(tc.tile_pool(name="lists", bufs=1))
+        sb = ctx.enter_context(tc.tile_pool(name="sb", bufs=1))
+        psum = ctx.enter_context(tc.psum_pool(name="psum", bufs=1))
+
+        def tile(tag, cols, dtype):
+            return sb.tile([P, cols], dtype, name=tag, tag=tag, align_bytes=64)
+
+        def bank(k):
+            return psum.tile([P, HALF], F32, name="bank%d" % k, tag="bank%d" % k)
+
+        def rows_4p(src):
+            return src.rearrange("(p j) c -> p j c", j=PACK)
+
+        def quantize(codes, scales, staged, first, count):
+            nc.vector.quantize_mx(out=codes[:, first:first + count].bitcast(FP8X4),
+                                  scales=scales[:, first:first + count],
+                                  in_=staged[:, PACK * first:PACK * (first + count)])
+
+        idx = lists.tile([P, S // 16], U16, name="idx")
+        idx2 = lists.tile([P, S // 16], U16, name="idx2")
+        idx3 = lists.tile([P, PCOLS // 16], U16, name="idx3")
+        table = [tile("big%d" % a, T, I32) for a in range(2)]
+        table_sc = tile("table_sc", T, U8)
+        nc.vector.memset(table_sc[:].bitcast(I32), 0)
+        for q in range(4):
+            nc.gpsimd.dma_start(out=table_sc[32 * q:32 * q + 8, :].bitcast(I32),
+                                in_=tab_scales[:, 4 * q:4 * q + 4, :].bitcast(I32))
+
+        def load_table(a):
+            nc.sync.dma_start(out=table[a][:], in_=tab_words[a].rearrange("p t i -> p (t i)").bitcast(I32))
+
+        def load_rows(slot, src, a, cols):
+            width = cols.stop - cols.start
+            raw = tile("raw%d" % slot, PACK * width, F32)
+            nc.sync.dma_start(out=raw[:].rearrange("p (j c) -> p j c", j=PACK),
+                              in_=rows_4p(src[a * PASS:(a + 1) * PASS, cols]))
+            return raw
+
+        w1_raw = {}
+        load_table(0)
+        nc.sync.dma_start(out=idx[:], in_=offs)
+        w1_raw[0, 0] = load_rows(0, w1, 0, slice(0, PASS))
+        load_table(1)
+        w1_raw[1, 0] = load_rows(1, w1, 1, slice(0, PASS))
+        wgs_sb = tile("wgs", S, F32)
+        nc.sync.dma_start(out=wgs_sb[:], in_=wgs)
+        nc.sync.dma_start(out=idx2[:], in_=offs2)
+        gain_sb = tile("gain", 2 * PACK, F32)
+        nc.sync.dma_start(out=gain_sb[:].rearrange("p (b i) -> p b i", i=PACK),
+                          in_=gain.rearrange("(b p i) -> p b i", p=P, i=PACK))
+        w1_raw[0, 1] = load_rows(2, w1, 0, slice(PASS, 2 * PASS))
+        w1_raw[1, 1] = load_rows(3, w1, 1, slice(PASS, 2 * PASS))
+
+        warm = tile("warm", 8, F32)
+        nc.vector.memset(warm[:], 0.0)
+        nc.scalar.activation(out=warm[:, 0:1], in_=warm[:, 1:2], func=ACT.Tanh)
+
+        pages = [tile("page%d" % i, T2, F32) for i in range(PACK)]
+        for i in range(PACK):
+            nc.vector.memset(pages[i][:], 0.0)
+        ident = tile("ident", P, F32)
+        make_identity(nc, ident[:])
+
+        v_words = [tile("v_words0", S, U32)]
+        v_sc = tile("v_sc", S, U8)
+        w1_stage = [tile("stage%d" % a, PACK * H, BF16) for a in range(2)]
+        w1_codes = [tile("codes%d" % a, H, U32) for a in range(2)]
+        w1_sc = [tile("scales%d" % a, H, U8) for a in range(2)]
+
+        def cast_w1(copy, a, b, first, count):
+            dst = w1_stage[a][:, b * PACK * PASS:(b + 1) * PACK * PASS].rearrange("p (t m j) -> p m t j", t=PACK, j=PACK)
+            src = w1_raw[a, b][:].rearrange("p (j m t) -> p m t j", j=PACK, t=PACK)
+            copy(out=dst[:, :, first:first + count, :], in_=src[:, :, first:first + count, :])
+
+        def quantize_w1(a, first, count):
+            quantize(w1_codes[a], w1_sc[a], w1_stage[a], first * P, count * P)
+
+        nc.vector.tensor_copy(v_words[0][:], table[0][:].bitcast(U32).indirect(idx[:]))
+        nc.vector.tensor_copy(v_sc[:], table_sc[:].indirect(idx[:]))
+        cast_w1(nc.scalar.copy, 0, 0, 0, PACK)
+        quantize_w1(0, 0, 1)
+        quantize_w1(0, 1, 2)
+        v_words.append(tile("table_sc", S, U32))
+        for c in range(2):
+            nc.vector.tensor_copy(v_words[1][:, c * HALF:(c + 1) * HALF],
+                                  table[1][:].bitcast(U32).indirect(idx[:, 32 * c:32 * (c + 1)]))
+        cast_w1(nc.vector.tensor_copy, 1, 0, 0, 1)
+        quantize_w1(1, 0, 1)
+        cast_w1(nc.vector.tensor_copy, 1, 0, 1, 2)
+        quantize_w1(1, 1, 2)
+
+        cloth_sb = []
+        wgt_sb = tile("wgt", PCOLS, F32)
+        nc.sync.dma_start(out=wgt_sb[:], in_=wgt)
+        nc.sync.dma_start(out=idx3[:], in_=offs3)
+
+        def load_cloth(b):
+            t = tile("big%d" % b, PACK * PCOLS, F32)
+            nc.sync.dma_start(out=t[:].rearrange("p (j c) -> p j c", j=PACK), in_=rows_4p(cloth[b * PASS:(b + 1) * PASS, :]))
+            cloth_sb.append(t)
+
+        h = [tile("h%d" % b, PACK * S, F32) for b in range(2)]
+
+        def make_h(s, pieces):
+            b, i = divmod(s, PACK)
+            for c in range(2):
+                acc = bank((2 * s + c) % 4)
+                for a in range(2):
+                    nc.tensor.matmul_mx(out=acc[:], lhsT=w1_codes[a][:, s * P:(s + 1) * P].bitcast(FP8X4),
+                                        lhsT_scale=w1_sc[a][:, s * P:(s + 1) * P],
+                                        rhs=v_words[a][:, c * HALF:(c + 1) * HALF].bitcast(FP8X4),
+                                        rhs_scale=v_sc[4 * a:P, c * HALF:(c + 1) * HALF], start=(a == 0), stop=(a == 1))
+                part = h[b][:, i * S + c * HALF:i * S + (c + 1) * HALF]
+                nc.scalar.activation(out=part, in_=acc[:], func=ACT.Tanh)
+                if pieces == 2:
+                    nc.scalar.activation(out=part, in_=part, func=ACT.Copy, scale=gain_sb[:, s:s + 1])
+            if pieces == 1:
+                row = h[b][:, i * S:(i + 1) * S]
+                nc.scalar.activation(out=row, in_=row, func=ACT.Copy, scale=gain_sb[:, s:s + 1])
+            width = S // pieces
+            for c in range(pieces):
+                nc.vector.tensor_tensor(pages[i][:].indirect(idx2[:, c * width // 16:(c + 1) * width // 16]),
+                                        h[b][:, i * S + c * width:i * S + (c + 1) * width],
+                                        wgs_sb[:, c * width:(c + 1) * width], ALU.mult)
+
+        def interleave(dst, src, width, first, count):
+            d = dst[:].rearrange("p (c i t) -> p c t i", i=PACK, t=PACK)
+            r = src[:].rearrange("p (t c i) -> p c t i", t=PACK, i=PACK)
+            nc.scalar.copy(out=d[:, first // PACK:(first + count) // PACK], in_=r[:, first // PACK:(first + count) // PACK])
+
+        def quantize_weight(name, src, slots, stage_tag):
+            staged = tile(stage_tag, 2 * PACK * N, BF16)
+            for b in range(2):
+                raw = load_rows(slots[b], src, b, slice(0, N))
+                nc.scalar.copy(out=staged[:, b * PACK * N:(b + 1) * PACK * N].rearrange("p (c i t) -> p c t i", i=PACK, t=PACK),
+                               in_=raw[:].rearrange("p (t c i) -> p c t i", t=PACK, i=PACK))
+            codes = tile(name + "_codes", 2 * N, U32)
+            scales = tile(name + "_sc", 2 * N, U8)
+            quantize(codes, scales, staged, 0, 512)
+            quantize(codes, scales, staged, 512, 256)
+            return codes, scales
+
+        h_codes = [tile("h_codes%d" % b, S, U32) for b in range(2)]
+        h_sc = [tile("h_sc%d" % b, S, U8) for b in range(2)]
+
+        def quantize_h(b):
+            staged = tile("stage%d" % b, PACK * S, BF16)
+            for c in range(2):
+                interleave(staged, h[b], S, c * HALF, HALF)
+            quantize(h_codes[b], h_sc[b], staged, 0, S)
+
+        def gather(x, i, first, count):
+            nc.vector.tensor_tensor(x[:, i * PCOLS + first:i * PCOLS + first + count],
+                                    pages[i][:].indirect(idx3[:, first // 16:(first + count) // 16]),
+                                    wgt_sb[:, first:first + count], ALU.mult)
+
+        def transpose_into(acc, src, i, jt, start, stop):
+            nc.tensor.matmul(acc[:, i * P:(i + 1) * P], lhsT=src[:, i * PCOLS + jt * P:i * PCOLS + (jt + 1) * P],
+                             rhs=ident[:], is_transpose=True, start=start, stop=stop)
+
+        def open_sum(b, jt):
+            acc = bank(jt % 4)
+            for i in range(PACK):
+                transpose_into(acc, cloth_sb[b], i, jt, i == 0, False)
+            return acc
+
+        def round_sum(acc, jt):
+            turned = tile("turned%d" % (jt % 4), PASS, BF16)
+            nc.scalar.copy(out=turned[:].rearrange("j (u p e) -> j u p e", u=2, e=2),
+                           in_=acc[:].rearrange("j (u e p) -> j u p e", u=2, e=2))
+            return turned
+
+        def turn_back(staged, pair, jt):
+            back = bank(4 + (jt // 2) % 2)
+            for t in range(2):
+                words = pair[t][:].bitcast(F32)
+                for u in range(2):
+                    nc.tensor.transpose(back[:, (2 * t + u) * P:(2 * t + u + 1) * P], words[:, u * P:(u + 1) * P], ident[:])
+            nc.scalar.copy(out=staged[:].bitcast(F32)[:, 2 * jt * P:2 * (jt + 2) * P].rearrange("p (t j u) -> p t j u", t=2, u=2),
+                           in_=back[:].rearrange("p (t u j) -> p t j u", t=2, u=2))
+
+        make_h(0, 2)
+        make_h(1, 1)
+        make_h(2, 1)
+        cast_w1(nc.scalar.copy, 1, 0, 3, 1)
+        for a in range(2):
+            cast_w1(nc.scalar.copy, a, 1, 0, PACK)
+        for a in range(2):
+            quantize_w1(a, 7, 1)
+            quantize_w1(a, 3, 4)
+        make_h(3, 1)
+        load_cloth(0)
+        wc_codes, wc_sc = quantize_weight("wc", wc, (0, 1), "stage2")
+        quantize_h(0)
+        x0 = tile("h0", PACK * PCOLS, F32)
+        for i in range(PACK):
+            gather(x0, i, 0, PCOLS)
+
+        for s in range(PACK, 2 * PACK):
+            make_h(s, 1)
+        wb_codes, wb_sc = quantize_weight("wb", wb, (2, 3), "stage3")
+        load_cloth(1)
+        wa_codes = tile("wa_codes", 2 * 2 * N, U8)
+        nc.sync.dma_start(out=wa_codes[:].rearrange("p (a n) -> p a n", a=2).bitcast(I32),
+                          in_=wa_words.rearrange("a p n -> p a n").bitcast(I32))
+        wa_sc = tile("wa_sc", 2 * N, U8)
+        nc.gpsimd.memset(wa_sc[:], 0)
+        for q in range(4):
+            nc.sync.dma_start(out=wa_sc[32 * q:32 * q + 4, :].rearrange("r (a n) -> r a n", a=2).bitcast(I32),
+                              in_=wa_scales[:, 4 * q:4 * q + 4, :].rearrange("a r n -> r a n").bitcast(I32))
+        cap_sb = tile("cap", N // P, F32)
+        with nc.allow_non_contiguous_dma(reason="one value of cap for each partition"):
+            nc.sync.dma_start(out=cap_sb[:], in_=cap.rearrange("(t p) -> p t", p=P))
+
+        z_codes = [tile("codes%d" % b, PCOLS, U32) for b in range(2)]
+        z_sc = [tile("scales%d" % b, PCOLS, U8) for b in range(2)]
+        z_stage = [tile("stage%d" % (2 + b), PACK * PCOLS, BF16) for b in range(2)]
+        for jp in range(0, PCOLS // P, 2):
+            pair = []
+            for jt in (jp, jp + 1):
+                acc = open_sum(0, jt)
+                for i in range(PACK):
+                    transpose_into(acc, x0, i, jt, False, i == PACK - 1)
+                pair.append(round_sum(acc, jt))
+            turn_back(z_stage[0], pair, jp)
+        quantize(z_codes[0], z_sc[0], z_stage[0], 0, PCOLS)
+
+        sums = [open_sum(1, jt) for jt in range(4)]
+        quantize_h(1)
+        yc = [tile("raw%d" % c, (N // P) * HALF, F32) for c in range(2)]
+        for c in range(2):
+            for nt in range(N // P):
+                acc = bank(6 + (3 * c + nt) % 2)
+                for b in range(2):
+                    w = slice(b * N + nt * P, b * N + (nt + 1) * P)
+                    nc.tensor.matmul_mx(out=acc[:], lhsT=wc_codes[:, w].bitcast(FP8X4), lhsT_scale=wc_sc[:, w],
+                                        rhs=h_codes[b][:, c * HALF:(c + 1) * HALF].bitcast(FP8X4),
+                                        rhs_scale=h_sc[b][:, c * HALF:(c + 1) * HALF], start=(b == 0), stop=(b == 1))
+                nc.scalar.activation(out=yc[c][:, nt * HALF:(nt + 1) * HALF], in_=acc[:], func=ACT.Identity,
+                                     bias=cap_sb[:, nt:nt + 1])
+
+        x1 = tile("h1", PACK * PCOLS, F32)
+        for i in range(PACK):
+            gather(x1, i, 0, HALF)
+            for jt in range(4):
+                transpose_into(sums[jt], x1, i, jt, False, i == PACK - 1)
+        for i in range(PACK):
+            gather(x1, i, HALF, HALF)
+        for jp in range(0, 4, 2):
+            turn_back(z_stage[1], [round_sum(sums[jt], jt) for jt in (jp, jp + 1)], jp)
+        quantize(z_codes[1], z_sc[1], z_stage[1], 0, HALF)
+
+        walk = slice(HALF // PACK, PCOLS // PACK)
+        nc.vector.tensor_tensor(z_stage[1][:].rearrange("p (c i t) -> p c t i", i=PACK, t=PACK)[:, walk],
+                                x1[:].rearrange("p (t c i) -> p c t i", t=PACK, i=PACK)[:, walk],
+                                cloth_sb[1][:].rearrange("p (t c i) -> p c t i", t=PACK, i=PACK)[:, walk], ALU.add)
+        quantize(z_codes[1], z_sc[1], z_stage[1], HALF, HALF)
+
+        scratch = tile("h0", PACK * PCOLS, F32)
+        out_banks = (6, 0, 2, 4, 6, 0)
+        for c in range(2):
+            cols = slice(c * HALF, (c + 1) * HALF)
+            for nt in range(N // P):
+                k = 3 * c + nt
+                ya = bank(out_banks[k])
+                yb = bank(out_banks[k] + 1)
+                for b in range(2):
+                    w = slice(b * N + nt * P, b * N + (nt + 1) * P)
+                    nc.tensor.matmul_mx(out=ya[:], lhsT=wa_codes[:, 2 * w.start:2 * w.stop].bitcast(FP4X4),
+                                        lhsT_scale=wa_sc[:, w], rhs=z_codes[b][:, cols].bitcast(FP8X4),
+                                        rhs_scale=z_sc[b][:, cols], start=(b == 0), stop=(b == 1))
+                for b in range(2):
+                    w = slice(b * N + nt * P, b * N + (nt + 1) * P)
+                    nc.tensor.matmul_mx(out=yb[:], lhsT=wb_codes[:, w].bitcast(FP8X4), lhsT_scale=wb_sc[:, w],
+                                        rhs=z_codes[b][:, cols].bitcast(FP8X4), rhs_scale=z_sc[b][:, cols],
+                                        start=(b == 0), stop=(b == 1))
+                larger = scratch[:, k * HALF:(k + 1) * HALF]
+                nc.scalar.copy(out=larger, in_=ya[:])
+                nc.vector.tensor_tensor(larger, larger, yb[:], ALU.max)
+                result = yc[c][:, nt * HALF:(nt + 1) * HALF]
+                nc.vector.tensor_tensor(result, larger, result, ALU.min)
+                nc.sync.dma_start(out=out[nt * P:(nt + 1) * P, cols], in_=result)

@@ -29,9 +29,19 @@ def tile_list_snooker_foul_review_kernel(tc, tab_words, tab_scales, offs, offs2,
     with ExitStack() as ctx:
         lists = ctx.enter_context(tc.tile_pool(name="lists", bufs=1))
         sb = ctx.enter_context(tc.tile_pool(name="sb", bufs=1))
+        later = ctx.enter_context(tc.tile_pool(name="later", bufs=1))
         psum = ctx.enter_context(tc.psum_pool(name="psum", bufs=1))
 
+        offsets = {}
+        total = 0
+        for tag, size in (("raw0", 8192), ("raw1", 8192), ("raw2", 8192), ("raw3", 8192), ("big1", 16384), ("wgs", 4096),
+                          ("wgt", 4096), ("wa_codes", 1536), ("gain", 64), ("cap", 64)):
+            offsets[tag] = total
+            total += size
+
         def tile(tag, cols, dtype):
+            if tag in offsets:
+                return later.tile([P, cols], dtype, name=tag, tag=tag, align_bytes=64, offset=offsets[tag])
             return sb.tile([P, cols], dtype, name=tag, tag=tag, align_bytes=64)
 
         def bank(k):
@@ -48,12 +58,12 @@ def tile_list_snooker_foul_review_kernel(tc, tab_words, tab_scales, offs, offs2,
         idx = lists.tile([P, S // 16], U16, name="idx")
         idx2 = lists.tile([P, S // 16], U16, name="idx2")
         idx3 = lists.tile([P, PCOLS // 16], U16, name="idx3")
-        table = [tile("big%d" % a, T, I32) for a in range(2)]
         table_sc = tile("table_sc", T, U8)
         nc.vector.memset(table_sc[:].bitcast(I32), 0)
-        for q in range(4):
-            nc.gpsimd.dma_start(out=table_sc[32 * q:32 * q + 8, :].bitcast(I32),
-                                in_=tab_scales[:, 4 * q:4 * q + 4, :].bitcast(I32))
+        warm = later.tile([P, total // 4], F32, name="warm", tag="warm", align_bytes=64, offset=0)
+        nc.vector.memset(warm[:, 0:8], 0.0)
+        nc.scalar.activation(out=warm[:, 0:1], in_=warm[:, 1:2], func=ACT.Tanh)
+        table = [tile("big%d" % a, T, I32) for a in range(2)]
 
         def load_table(a):
             nc.sync.dma_start(out=table[a][:], in_=tab_words[a].rearrange("p t i -> p (t i)").bitcast(I32))
@@ -66,23 +76,23 @@ def tile_list_snooker_foul_review_kernel(tc, tab_words, tab_scales, offs, offs2,
             return raw
 
         w1_raw = {}
-        load_table(0)
         nc.sync.dma_start(out=idx[:], in_=offs)
+        nc.sync.dma_start(out=idx2[:], in_=offs2)
+        nc.sync.dma_start(out=idx3[:], in_=offs3)
+        load_table(0)
+        for q in range(4):
+            nc.sync.dma_start(out=table_sc[32 * q:32 * q + 8, :].bitcast(I32),
+                              in_=tab_scales[:, 4 * q:4 * q + 4, :].bitcast(I32))
         w1_raw[0, 0] = load_rows(0, w1, 0, slice(0, PASS))
         load_table(1)
         w1_raw[1, 0] = load_rows(1, w1, 1, slice(0, PASS))
         wgs_sb = tile("wgs", S, F32)
         nc.sync.dma_start(out=wgs_sb[:], in_=wgs)
-        nc.sync.dma_start(out=idx2[:], in_=offs2)
         gain_sb = tile("gain", 2 * PACK, F32)
         nc.sync.dma_start(out=gain_sb[:].rearrange("p (b i) -> p b i", i=PACK),
                           in_=gain.rearrange("(b p i) -> p b i", p=P, i=PACK))
         w1_raw[0, 1] = load_rows(2, w1, 0, slice(PASS, 2 * PASS))
         w1_raw[1, 1] = load_rows(3, w1, 1, slice(PASS, 2 * PASS))
-
-        warm = tile("warm", 8, F32)
-        nc.vector.memset(warm[:], 0.0)
-        nc.scalar.activation(out=warm[:, 0:1], in_=warm[:, 1:2], func=ACT.Tanh)
 
         pages = [tile("page%d" % i, T2, F32) for i in range(PACK)]
         for i in range(PACK):
@@ -121,7 +131,6 @@ def tile_list_snooker_foul_review_kernel(tc, tab_words, tab_scales, offs, offs2,
         cloth_sb = []
         wgt_sb = tile("wgt", PCOLS, F32)
         nc.sync.dma_start(out=wgt_sb[:], in_=wgt)
-        nc.sync.dma_start(out=idx3[:], in_=offs3)
 
         def load_cloth(b):
             t = tile("big%d" % b, PACK * PCOLS, F32)
@@ -233,7 +242,7 @@ def tile_list_snooker_foul_review_kernel(tc, tab_words, tab_scales, offs, offs2,
         nc.sync.dma_start(out=wa_codes[:].rearrange("p (a n) -> p a n", a=2).bitcast(I32),
                           in_=wa_words.rearrange("a p n -> p a n").bitcast(I32))
         wa_sc = tile("wa_sc", 2 * N, U8)
-        nc.gpsimd.memset(wa_sc[:], 0)
+        nc.vector.memset(wa_sc[:].bitcast(I32), 0)
         for q in range(4):
             nc.sync.dma_start(out=wa_sc[32 * q:32 * q + 4, :].rearrange("r (a n) -> r a n", a=2).bitcast(I32),
                               in_=wa_scales[:, 4 * q:4 * q + 4, :].rearrange("a r n -> r a n").bitcast(I32))

@@ -35,9 +35,10 @@ def tile_list_snooker_foul_review_kernel(tc, tab_words, tab_scales, offs, offs2,
         offsets = {}
         total = 0
         for tag, size in (("raw0", 8192), ("raw1", 8192), ("raw2", 8192), ("raw3", 8192), ("big1", 16384), ("wgs", 4096),
-                          ("wgt", 4096), ("wa_codes", 1536), ("gain", 64), ("cap", 64)):
+                          ("wgt", 4096), ("wa_codes", 1536), ("wa_sc", 768), ("gain", 64), ("cap", 64)):
             offsets[tag] = total
             total += size
+        offsets["x0"] = offsets["raw2"]
 
         def tile(tag, cols, dtype):
             if tag in offsets:
@@ -77,20 +78,20 @@ def tile_list_snooker_foul_review_kernel(tc, tab_words, tab_scales, offs, offs2,
 
         w1_raw = {}
         nc.sync.dma_start(out=idx[:], in_=offs)
+        load_table(0)
         nc.sync.dma_start(out=idx2[:], in_=offs2)
         nc.sync.dma_start(out=idx3[:], in_=offs3)
-        load_table(0)
         for q in range(4):
             nc.sync.dma_start(out=table_sc[32 * q:32 * q + 8, :].bitcast(I32),
                               in_=tab_scales[:, 4 * q:4 * q + 4, :].bitcast(I32))
         w1_raw[0, 0] = load_rows(0, w1, 0, slice(0, PASS))
         load_table(1)
         w1_raw[1, 0] = load_rows(1, w1, 1, slice(0, PASS))
-        wgs_sb = tile("wgs", S, F32)
-        nc.sync.dma_start(out=wgs_sb[:], in_=wgs)
         gain_sb = tile("gain", 2 * PACK, F32)
         nc.sync.dma_start(out=gain_sb[:].rearrange("p (b i) -> p b i", i=PACK),
                           in_=gain.rearrange("(b p i) -> p b i", p=P, i=PACK))
+        wgs_sb = tile("wgs", S, F32)
+        nc.sync.dma_start(out=wgs_sb[:], in_=wgs)
         w1_raw[0, 1] = load_rows(2, w1, 0, slice(PASS, 2 * PASS))
         w1_raw[1, 1] = load_rows(3, w1, 1, slice(PASS, 2 * PASS))
 
@@ -117,16 +118,17 @@ def tile_list_snooker_foul_review_kernel(tc, tab_words, tab_scales, offs, offs2,
         nc.vector.tensor_copy(v_words[0][:], table[0][:].bitcast(U32).indirect(idx[:]))
         nc.vector.tensor_copy(v_sc[:], table_sc[:].indirect(idx[:]))
         cast_w1(nc.scalar.copy, 0, 0, 0, PACK)
-        quantize_w1(0, 0, 1)
-        quantize_w1(0, 1, 2)
+        quantize_w1(0, 0, PACK)
         v_words.append(tile("table_sc", S, U32))
         for c in range(2):
             nc.vector.tensor_copy(v_words[1][:, c * HALF:(c + 1) * HALF],
                                   table[1][:].bitcast(U32).indirect(idx[:, 32 * c:32 * (c + 1)]))
         cast_w1(nc.vector.tensor_copy, 1, 0, 0, 1)
         quantize_w1(1, 0, 1)
-        cast_w1(nc.vector.tensor_copy, 1, 0, 1, 2)
-        quantize_w1(1, 1, 2)
+        cast_w1(nc.vector.tensor_copy, 1, 0, 1, 1)
+        quantize_w1(1, 1, 1)
+        cast_w1(nc.scalar.copy, 1, 0, 2, 2)
+        quantize_w1(1, 2, 2)
 
         cloth_sb = []
         wgt_sb = tile("wgt", PCOLS, F32)
@@ -139,27 +141,29 @@ def tile_list_snooker_foul_review_kernel(tc, tab_words, tab_scales, offs, offs2,
 
         h = [tile("h%d" % b, PACK * S, F32) for b in range(2)]
 
-        def make_h(s, pieces):
+        def h_cols(s, first, count):
             b, i = divmod(s, PACK)
+            return h[b][:, i * S + first:i * S + first + count]
+
+        def bounded(s, first, count, k):
+            acc = bank(k % 4)
+            cols = slice(first, first + count)
+            for a in range(2):
+                nc.tensor.matmul_mx(out=acc[:, 0:count], lhsT=w1_codes[a][:, s * P:(s + 1) * P].bitcast(FP8X4),
+                                    lhsT_scale=w1_sc[a][:, s * P:(s + 1) * P], rhs=v_words[a][:, cols].bitcast(FP8X4),
+                                    rhs_scale=v_sc[4 * a:P, cols], start=(a == 0), stop=(a == 1))
+            nc.scalar.activation(out=h_cols(s, first, count), in_=acc[:, 0:count], func=ACT.Tanh)
+
+        def file_h(s, first, count):
+            part = h_cols(s, first, count)
+            nc.scalar.activation(out=part, in_=part, func=ACT.Copy, scale=gain_sb[:, s:s + 1])
+            nc.vector.tensor_tensor(pages[s % PACK][:].indirect(idx2[:, first // 16:(first + count) // 16]), part,
+                                    wgs_sb[:, first:first + count], ALU.mult)
+
+        def make_h(s):
             for c in range(2):
-                acc = bank((2 * s + c) % 4)
-                for a in range(2):
-                    nc.tensor.matmul_mx(out=acc[:], lhsT=w1_codes[a][:, s * P:(s + 1) * P].bitcast(FP8X4),
-                                        lhsT_scale=w1_sc[a][:, s * P:(s + 1) * P],
-                                        rhs=v_words[a][:, c * HALF:(c + 1) * HALF].bitcast(FP8X4),
-                                        rhs_scale=v_sc[4 * a:P, c * HALF:(c + 1) * HALF], start=(a == 0), stop=(a == 1))
-                part = h[b][:, i * S + c * HALF:i * S + (c + 1) * HALF]
-                nc.scalar.activation(out=part, in_=acc[:], func=ACT.Tanh)
-                if pieces == 2:
-                    nc.scalar.activation(out=part, in_=part, func=ACT.Copy, scale=gain_sb[:, s:s + 1])
-            if pieces == 1:
-                row = h[b][:, i * S:(i + 1) * S]
-                nc.scalar.activation(out=row, in_=row, func=ACT.Copy, scale=gain_sb[:, s:s + 1])
-            width = S // pieces
-            for c in range(pieces):
-                nc.vector.tensor_tensor(pages[i][:].indirect(idx2[:, c * width // 16:(c + 1) * width // 16]),
-                                        h[b][:, i * S + c * width:i * S + (c + 1) * width],
-                                        wgs_sb[:, c * width:(c + 1) * width], ALU.mult)
+                bounded(s, c * HALF, HALF, 2 * s + c + 1)
+            file_h(s, 0, S)
 
         def interleave(dst, src, width, first, count):
             d = dst[:].rearrange("p (c i t) -> p c t i", i=PACK, t=PACK)
@@ -208,35 +212,39 @@ def tile_list_snooker_foul_review_kernel(tc, tab_words, tab_scales, offs, offs2,
                            in_=acc[:].rearrange("j (u e p) -> j u p e", u=2, e=2))
             return turned
 
-        def turn_back(staged, pair, jt):
+        def turn_back(staged, turned, jt):
             back = bank(4 + (jt // 2) % 2)
-            for t in range(2):
-                words = pair[t][:].bitcast(F32)
+            count = len(turned)
+            for t in range(count):
+                words = turned[t][:].bitcast(F32)
                 for u in range(2):
                     nc.tensor.transpose(back[:, (2 * t + u) * P:(2 * t + u + 1) * P], words[:, u * P:(u + 1) * P], ident[:])
-            nc.scalar.copy(out=staged[:].bitcast(F32)[:, 2 * jt * P:2 * (jt + 2) * P].rearrange("p (t j u) -> p t j u", t=2, u=2),
-                           in_=back[:].rearrange("p (t u j) -> p t j u", t=2, u=2))
+            nc.scalar.copy(out=staged[:].bitcast(F32)[:, 2 * jt * P:2 * (jt + count) * P].rearrange("p (t j u) -> p t j u", t=count, u=2),
+                           in_=back[:, 0:2 * count * P].rearrange("p (t u j) -> p t j u", t=count, u=2))
 
-        make_h(0, 2)
-        make_h(1, 1)
-        make_h(2, 1)
-        cast_w1(nc.scalar.copy, 1, 0, 3, 1)
+        bounded(0, 0, 256, 0)
+        file_h(0, 0, 256)
+        bounded(1, 0, HALF, 1)
+        file_h(1, 0, HALF)
+        bounded(0, 256, 256, 2)
+        bounded(0, HALF, HALF, 3)
+        file_h(0, 256, 768)
+        bounded(1, HALF, HALF, 4)
+        file_h(1, HALF, HALF)
         for a in range(2):
             cast_w1(nc.scalar.copy, a, 1, 0, PACK)
-        for a in range(2):
-            quantize_w1(a, 7, 1)
-            quantize_w1(a, 3, 4)
-        make_h(3, 1)
+            quantize_w1(a, PACK, PACK)
+            make_h(2 + a)
         load_cloth(0)
-        wc_codes, wc_sc = quantize_weight("wc", wc, (0, 1), "stage2")
-        quantize_h(0)
-        x0 = tile("h0", PACK * PCOLS, F32)
+        x0 = tile("x0", PACK * PCOLS, F32)
         for i in range(PACK):
             gather(x0, i, 0, PCOLS)
 
+        wc_codes, wc_sc = quantize_weight("wc", wc, (0, 1), "stage2")
+        quantize_h(0)
+        wb_codes, wb_sc = quantize_weight("wb", wb, (0, 1), "stage3")
         for s in range(PACK, 2 * PACK):
-            make_h(s, 1)
-        wb_codes, wb_sc = quantize_weight("wb", wb, (2, 3), "stage3")
+            make_h(s)
         load_cloth(1)
         wa_codes = tile("wa_codes", 2 * 2 * N, U8)
         nc.sync.dma_start(out=wa_codes[:].rearrange("p (a n) -> p a n", a=2).bitcast(I32),
@@ -282,26 +290,43 @@ def tile_list_snooker_foul_review_kernel(tc, tab_words, tab_scales, offs, offs2,
             gather(x1, i, 0, HALF)
             for jt in range(4):
                 transpose_into(sums[jt], x1, i, jt, False, i == PACK - 1)
-        for i in range(PACK):
-            gather(x1, i, HALF, HALF)
         for jp in range(0, 4, 2):
             turn_back(z_stage[1], [round_sum(sums[jt], jt) for jt in (jp, jp + 1)], jp)
+        sums = {jt: open_sum(1, jt) for jt in range(4, 7)}
+        for i in range(PACK):
+            gather(x1, i, HALF, 3 * P)
+            for jt in range(4, 7):
+                transpose_into(sums[jt], x1, i, jt, False, i == PACK - 1)
         quantize(z_codes[1], z_sc[1], z_stage[1], 0, HALF)
+        for i in range(PACK):
+            gather(x1, i, 7 * P, P)
+        turn_back(z_stage[1], [round_sum(sums[jt], jt) for jt in (4, 5)], 4)
+        turn_back(z_stage[1], [round_sum(sums[6], 6)], 6)
 
-        walk = slice(HALF // PACK, PCOLS // PACK)
+        walk = slice(7 * P // PACK, PCOLS // PACK)
         nc.vector.tensor_tensor(z_stage[1][:].rearrange("p (c i t) -> p c t i", i=PACK, t=PACK)[:, walk],
                                 x1[:].rearrange("p (t c i) -> p c t i", t=PACK, i=PACK)[:, walk],
                                 cloth_sb[1][:].rearrange("p (t c i) -> p c t i", t=PACK, i=PACK)[:, walk], ALU.add)
-        quantize(z_codes[1], z_sc[1], z_stage[1], HALF, HALF)
 
         scratch = tile("h0", PACK * PCOLS, F32)
-        out_banks = (6, 0, 2, 4, 6, 0)
+        out_banks = ((6, 7), (3, 0), (6, 7), (1, 2), (4, 5), (3, 0))
+
+        def finish(k, pieces):
+            c, nt = divmod(k, N // P)
+            width = HALF // pieces
+            for first in range(0, HALF, width):
+                result = yc[c][:, nt * HALF + first:nt * HALF + first + width]
+                nc.vector.tensor_tensor(result, scratch[:, k * HALF + first:k * HALF + first + width], result, ALU.min)
+                nc.sync.dma_start(out=out[nt * P:(nt + 1) * P, c * HALF + first:c * HALF + first + width], in_=result)
+
         for c in range(2):
             cols = slice(c * HALF, (c + 1) * HALF)
+            if c == 1:
+                quantize(z_codes[1], z_sc[1], z_stage[1], HALF, HALF)
             for nt in range(N // P):
                 k = 3 * c + nt
-                ya = bank(out_banks[k])
-                yb = bank(out_banks[k] + 1)
+                ya = bank(out_banks[k][0])
+                yb = bank(out_banks[k][1])
                 for b in range(2):
                     w = slice(b * N + nt * P, b * N + (nt + 1) * P)
                     nc.tensor.matmul_mx(out=ya[:], lhsT=wa_codes[:, 2 * w.start:2 * w.stop].bitcast(FP4X4),
@@ -315,6 +340,6 @@ def tile_list_snooker_foul_review_kernel(tc, tab_words, tab_scales, offs, offs2,
                 larger = scratch[:, k * HALF:(k + 1) * HALF]
                 nc.scalar.copy(out=larger, in_=ya[:])
                 nc.vector.tensor_tensor(larger, larger, yb[:], ALU.max)
-                result = yc[c][:, nt * HALF:(nt + 1) * HALF]
-                nc.vector.tensor_tensor(result, larger, result, ALU.min)
-                nc.sync.dma_start(out=out[nt * P:(nt + 1) * P, cols], in_=result)
+                if k > 0:
+                    finish(k - 1, 1)
+        finish(5, 2)

@@ -85,8 +85,8 @@ def tile_list_snooker_foul_review_kernel(tc, tab_words, tab_scales, offs, offs2,
             nc.sync.dma_start(out=table_sc[32 * q:32 * q + 8, :].bitcast(I32),
                               in_=tab_scales[:, 4 * q:4 * q + 4, :].bitcast(I32))
         w1_raw[0, 0] = load_rows(0, w1, 0, slice(0, PASS))
-        load_table(1)
         w1_raw[1, 0] = load_rows(1, w1, 1, slice(0, PASS))
+        load_table(1)
         gain_sb = tile("gain", 2 * PACK, F32)
         nc.sync.dma_start(out=gain_sb[:].rearrange("p (b i) -> p b i", i=PACK),
                           in_=gain.rearrange("(b p i) -> p b i", p=P, i=PACK))
@@ -95,11 +95,12 @@ def tile_list_snooker_foul_review_kernel(tc, tab_words, tab_scales, offs, offs2,
         w1_raw[0, 1] = load_rows(2, w1, 0, slice(PASS, 2 * PASS))
         w1_raw[1, 1] = load_rows(3, w1, 1, slice(PASS, 2 * PASS))
 
+        ident = tile("ident", P, F32)
         pages = [tile("page%d" % i, T2, F32) for i in range(PACK)]
         for i in range(PACK):
-            nc.vector.memset(pages[i][:], 0.0)
-        ident = tile("ident", P, F32)
-        make_identity(nc, ident[:])
+            if i == 2:
+                make_identity(nc, ident[:])
+            (nc.vector if i < 2 else nc.gpsimd).memset(pages[i][:], 0.0)
 
         v_words = [tile("v_words0", S, U32)]
         v_sc = tile("v_sc", S, U8)
@@ -119,16 +120,12 @@ def tile_list_snooker_foul_review_kernel(tc, tab_words, tab_scales, offs, offs2,
         nc.vector.tensor_copy(v_sc[:], table_sc[:].indirect(idx[:]))
         cast_w1(nc.scalar.copy, 0, 0, 0, PACK)
         quantize_w1(0, 0, PACK)
+        cast_w1(nc.vector.tensor_copy, 1, 0, 0, PACK)
+        quantize_w1(1, 0, PACK)
         v_words.append(tile("table_sc", S, U32))
         for c in range(2):
             nc.vector.tensor_copy(v_words[1][:, c * HALF:(c + 1) * HALF],
                                   table[1][:].bitcast(U32).indirect(idx[:, 32 * c:32 * (c + 1)]))
-        cast_w1(nc.vector.tensor_copy, 1, 0, 0, 1)
-        quantize_w1(1, 0, 1)
-        cast_w1(nc.vector.tensor_copy, 1, 0, 1, 1)
-        quantize_w1(1, 1, 1)
-        cast_w1(nc.scalar.copy, 1, 0, 2, 2)
-        quantize_w1(1, 2, 2)
 
         cloth_sb = []
         wgt_sb = tile("wgt", PCOLS, F32)
@@ -154,9 +151,12 @@ def tile_list_snooker_foul_review_kernel(tc, tab_words, tab_scales, offs, offs2,
                                     rhs_scale=v_sc[4 * a:P, cols], start=(a == 0), stop=(a == 1))
             nc.scalar.activation(out=h_cols(s, first, count), in_=acc[:, 0:count], func=ACT.Tanh)
 
-        def file_h(s, first, count):
+        def file_h(s, first, count, on_vector=False):
             part = h_cols(s, first, count)
-            nc.scalar.activation(out=part, in_=part, func=ACT.Copy, scale=gain_sb[:, s:s + 1])
+            if on_vector:
+                nc.vector.tensor_scalar_mul(part, part, gain_sb[:, s:s + 1])
+            else:
+                nc.scalar.activation(out=part, in_=part, func=ACT.Copy, scale=gain_sb[:, s:s + 1])
             nc.vector.tensor_tensor(pages[s % PACK][:].indirect(idx2[:, first // 16:(first + count) // 16]), part,
                                     wgs_sb[:, first:first + count], ALU.mult)
 
@@ -185,11 +185,11 @@ def tile_list_snooker_foul_review_kernel(tc, tab_words, tab_scales, offs, offs2,
         h_codes = [tile("h_codes%d" % b, S, U32) for b in range(2)]
         h_sc = [tile("h_sc%d" % b, S, U8) for b in range(2)]
 
-        def quantize_h(b):
+        def round_h(b):
             staged = tile("stage%d" % b, PACK * S, BF16)
             for c in range(2):
                 interleave(staged, h[b], S, c * HALF, HALF)
-            quantize(h_codes[b], h_sc[b], staged, 0, S)
+            return staged
 
         def gather(x, i, first, count):
             nc.vector.tensor_tensor(x[:, i * PCOLS + first:i * PCOLS + first + count],
@@ -212,18 +212,18 @@ def tile_list_snooker_foul_review_kernel(tc, tab_words, tab_scales, offs, offs2,
                            in_=acc[:].rearrange("j (u e p) -> j u p e", u=2, e=2))
             return turned
 
-        def turn_back(staged, turned, jt):
+        def turn_back(staged, turned, jt, at):
             back = bank(4 + (jt // 2) % 2)
             count = len(turned)
             for t in range(count):
                 words = turned[t][:].bitcast(F32)
                 for u in range(2):
                     nc.tensor.transpose(back[:, (2 * t + u) * P:(2 * t + u + 1) * P], words[:, u * P:(u + 1) * P], ident[:])
-            nc.scalar.copy(out=staged[:].bitcast(F32)[:, 2 * jt * P:2 * (jt + count) * P].rearrange("p (t j u) -> p t j u", t=count, u=2),
+            nc.scalar.copy(out=staged[:].bitcast(F32)[:, 2 * at * P:2 * (at + count) * P].rearrange("p (t j u) -> p t j u", t=count, u=2),
                            in_=back[:, 0:2 * count * P].rearrange("p (t u j) -> p t j u", t=count, u=2))
 
         bounded(0, 0, 256, 0)
-        file_h(0, 0, 256)
+        file_h(0, 0, 256, True)
         bounded(1, 0, HALF, 1)
         file_h(1, 0, HALF)
         bounded(0, 256, 256, 2)
@@ -241,7 +241,7 @@ def tile_list_snooker_foul_review_kernel(tc, tab_words, tab_scales, offs, offs2,
             gather(x0, i, 0, PCOLS)
 
         wc_codes, wc_sc = quantize_weight("wc", wc, (0, 1), "stage2")
-        quantize_h(0)
+        quantize(h_codes[0], h_sc[0], round_h(0), 0, S)
         wb_codes, wb_sc = quantize_weight("wb", wb, (0, 1), "stage3")
         for s in range(PACK, 2 * PACK):
             make_h(s)
@@ -260,7 +260,8 @@ def tile_list_snooker_foul_review_kernel(tc, tab_words, tab_scales, offs, offs2,
 
         z_codes = [tile("codes%d" % b, PCOLS, U32) for b in range(2)]
         z_sc = [tile("scales%d" % b, PCOLS, U8) for b in range(2)]
-        z_stage = [tile("stage%d" % (2 + b), PACK * PCOLS, BF16) for b in range(2)]
+        z0_stage = tile("stage2", PACK * PCOLS, BF16)
+        z1_stage = [tile("stage%d" % (4 - c), PACK * HALF, BF16) for c in range(2)]
         for jp in range(0, PCOLS // P, 2):
             pair = []
             for jt in (jp, jp + 1):
@@ -268,13 +269,14 @@ def tile_list_snooker_foul_review_kernel(tc, tab_words, tab_scales, offs, offs2,
                 for i in range(PACK):
                     transpose_into(acc, x0, i, jt, False, i == PACK - 1)
                 pair.append(round_sum(acc, jt))
-            turn_back(z_stage[0], pair, jp)
-        quantize(z_codes[0], z_sc[0], z_stage[0], 0, PCOLS)
+            turn_back(z0_stage, pair, jp, jp)
+        quantize(z_codes[0], z_sc[0], z0_stage, 0, PCOLS)
 
         sums = [open_sum(1, jt) for jt in range(4)]
-        quantize_h(1)
+        h1_stage = round_h(1)
         yc = [tile("raw%d" % c, (N // P) * HALF, F32) for c in range(2)]
-        for c in range(2):
+
+        def make_yc(c):
             for nt in range(N // P):
                 acc = bank(6 + (3 * c + nt) % 2)
                 for b in range(2):
@@ -285,28 +287,33 @@ def tile_list_snooker_foul_review_kernel(tc, tab_words, tab_scales, offs, offs2,
                 nc.scalar.activation(out=yc[c][:, nt * HALF:(nt + 1) * HALF], in_=acc[:], func=ACT.Identity,
                                      bias=cap_sb[:, nt:nt + 1])
 
+        quantize(h_codes[1], h_sc[1], h1_stage, 0, HALF)
+        make_yc(0)
         x1 = tile("h1", PACK * PCOLS, F32)
         for i in range(PACK):
             gather(x1, i, 0, HALF)
             for jt in range(4):
                 transpose_into(sums[jt], x1, i, jt, False, i == PACK - 1)
+        quantize(h_codes[1], h_sc[1], h1_stage, HALF, HALF)
         for jp in range(0, 4, 2):
-            turn_back(z_stage[1], [round_sum(sums[jt], jt) for jt in (jp, jp + 1)], jp)
+            turn_back(z1_stage[0], [round_sum(sums[jt], jt) for jt in (jp, jp + 1)], jp, jp)
+        make_yc(1)
         sums = {jt: open_sum(1, jt) for jt in range(4, 7)}
         for i in range(PACK):
             gather(x1, i, HALF, 3 * P)
             for jt in range(4, 7):
                 transpose_into(sums[jt], x1, i, jt, False, i == PACK - 1)
-        quantize(z_codes[1], z_sc[1], z_stage[1], 0, HALF)
+        quantize(z_codes[1], z_sc[1], z1_stage[0], 0, HALF)
+        x_last = tile("stage4", PACK * P, F32)
         for i in range(PACK):
-            gather(x1, i, 7 * P, P)
-        turn_back(z_stage[1], [round_sum(sums[jt], jt) for jt in (4, 5)], 4)
-        turn_back(z_stage[1], [round_sum(sums[6], 6)], 6)
+            nc.vector.tensor_tensor(x_last[:, i * P:(i + 1) * P], pages[i][:].indirect(idx3[:, 7 * P // 16:]),
+                                    wgt_sb[:, 7 * P:], ALU.mult)
+        turn_back(z1_stage[1], [round_sum(sums[jt], jt) for jt in (4, 5)], 4, 0)
+        turn_back(z1_stage[1], [round_sum(sums[6], 6)], 6, 2)
 
-        walk = slice(7 * P // PACK, PCOLS // PACK)
-        nc.vector.tensor_tensor(z_stage[1][:].rearrange("p (c i t) -> p c t i", i=PACK, t=PACK)[:, walk],
-                                x1[:].rearrange("p (t c i) -> p c t i", t=PACK, i=PACK)[:, walk],
-                                cloth_sb[1][:].rearrange("p (t c i) -> p c t i", t=PACK, i=PACK)[:, walk], ALU.add)
+        nc.vector.tensor_tensor(z1_stage[1][:, 3 * PASS:].rearrange("p (c i t) -> p c t i", i=PACK, t=PACK),
+                                x_last[:].rearrange("p (t c i) -> p c t i", t=PACK, i=PACK),
+                                cloth_sb[1][:].rearrange("p (t c i) -> p c t i", t=PACK, i=PACK)[:, 7 * P // PACK:], ALU.add)
 
         scratch = tile("h0", PACK * PCOLS, F32)
         out_banks = ((6, 7), (3, 0), (6, 7), (1, 2), (4, 5), (3, 0))
@@ -322,7 +329,7 @@ def tile_list_snooker_foul_review_kernel(tc, tab_words, tab_scales, offs, offs2,
         for c in range(2):
             cols = slice(c * HALF, (c + 1) * HALF)
             if c == 1:
-                quantize(z_codes[1], z_sc[1], z_stage[1], HALF, HALF)
+                nc.vector.quantize_mx(out=z_codes[1][:, HALF:].bitcast(FP8X4), scales=z_sc[1][:, HALF:], in_=z1_stage[1][:])
             for nt in range(N // P):
                 k = 3 * c + nt
                 ya = bank(out_banks[k][0])

from contextlib import ExitStack

import concourse.mybir as mybir
from concourse.masks import make_identity

K, T, S, H, T2, PCOLS, N = 1024, 4096, 1024, 1024, 2048, 1024, 384
FLOPS = 2 * K * H * S + 3 * 2 * H * N * PCOLS

F32 = mybir.dt.float32
BF16 = mybir.dt.bfloat16
I32 = mybir.dt.int32
U32 = mybir.dt.uint32
U16 = mybir.dt.uint16
U8 = mybir.dt.uint8
FP8X4 = mybir.dt.float8_e4m3fn_x4
FP4X4 = mybir.dt.float4_e2m1fn_x4
ALU = mybir.AluOpType
ACT = mybir.ActivationFunctionType

P = 128
PACK = 4
PASS = P * PACK
HALF = 512


def tile_list_snooker_foul_review_kernel(tc, tab_words, tab_scales, offs, offs2, offs3, wgs, wgt, w1, gain,
                                                   cloth, wa_words, wa_scales, wb, wc, cap, out):
    nc = tc.nc
    with ExitStack() as ctx:
        lists = ctx.enter_context(tc.tile_pool(name="lists", bufs=1))
        sb = ctx.enter_context(tc.tile_pool(name="sb", bufs=1))
        later = ctx.enter_context(tc.tile_pool(name="later", bufs=1))
        psum = ctx.enter_context(tc.psum_pool(name="psum", bufs=1))

        offsets = {}
        total = 0
        for tag, size in (("raw0", 8192), ("raw1", 8192), ("raw2", 8192), ("raw3", 8192), ("big1", 16384), ("wgs", 4096),
                          ("wgt", 4096), ("wa_codes", 1536), ("wa_sc", 768), ("gain", 64), ("cap", 64)):
            offsets[tag] = total
            total += size
        offsets["x0"] = offsets["raw2"]

        def tile(tag, cols, dtype):
            if tag in offsets:
                return later.tile([P, cols], dtype, name=tag, tag=tag, align_bytes=64, offset=offsets[tag])
            return sb.tile([P, cols], dtype, name=tag, tag=tag, align_bytes=64)

        def bank(k):
            return psum.tile([P, HALF], F32, name="bank%d" % k, tag="bank%d" % k)

        def rows_4p(src):
            return src.rearrange("(p j) c -> p j c", j=PACK)

        def quantize(codes, scales, staged, first, count):
            nc.vector.quantize_mx(out=codes[:, first:first + count].bitcast(FP8X4),
                                  scales=scales[:, first:first + count],
                                  in_=staged[:, PACK * first:PACK * (first + count)])

        idx = lists.tile([P, S // 16], U16, name="idx")
        idx2 = lists.tile([P, S // 16], U16, name="idx2")
        idx3 = lists.tile([P, PCOLS // 16], U16, name="idx3")
        table_sc = tile("table_sc", T, U8)
        nc.vector.memset(table_sc[:].bitcast(I32), 0)
        warm = later.tile([P, total // 4], F32, name="warm", tag="warm", align_bytes=64, offset=0)
        nc.vector.memset(warm[:, 0:8], 0.0)
        nc.scalar.activation(out=warm[:, 0:1], in_=warm[:, 1:2], func=ACT.Tanh)
        table = [tile("big%d" % a, T, I32) for a in range(2)]

        def load_table(a):
            nc.sync.dma_start(out=table[a][:], in_=tab_words[a].rearrange("p t i -> p (t i)").bitcast(I32))

        def load_rows(slot, src, a, cols):
            width = cols.stop - cols.start
            raw = tile("raw%d" % slot, PACK * width, F32)
            nc.sync.dma_start(out=raw[:].rearrange("p (j c) -> p j c", j=PACK),
                              in_=rows_4p(src[a * PASS:(a + 1) * PASS, cols]))
            return raw

        w1_raw = {}
        nc.sync.dma_start(out=idx[:], in_=offs)
        load_table(0)
        nc.sync.dma_start(out=idx2[:], in_=offs2)
        nc.sync.dma_start(out=idx3[:], in_=offs3)
        for q in range(4):
            nc.sync.dma_start(out=table_sc[32 * q:32 * q + 8, :].bitcast(I32),
                              in_=tab_scales[:, 4 * q:4 * q + 4, :].bitcast(I32))
        w1_raw[0, 0] = load_rows(0, w1, 0, slice(0, PASS))
        w1_raw[1, 0] = load_rows(1, w1, 1, slice(0, PASS))
        load_table(1)
        gain_sb = tile("gain", 2 * PACK, F32)
        nc.sync.dma_start(out=gain_sb[:].rearrange("p (b i) -> p b i", i=PACK),
                          in_=gain.rearrange("(b p i) -> p b i", p=P, i=PACK))
        wgs_sb = tile("wgs", S, F32)
        nc.sync.dma_start(out=wgs_sb[:], in_=wgs)
        w1_raw[0, 1] = load_rows(2, w1, 0, slice(PASS, 2 * PASS))
        w1_raw[1, 1] = load_rows(3, w1, 1, slice(PASS, 2 * PASS))

        ident = tile("ident", P, F32)
        pages = [tile("page%d" % i, T2, F32) for i in range(PACK)]
        for i in range(PACK):
            if i == 2:
                make_identity(nc, ident[:])
            (nc.vector if i < 2 else nc.gpsimd).memset(pages[i][:], 0.0)

        v_words = [tile("v_words0", S, U32)]
        v_sc = tile("v_sc", S, U8)
        w1_stage = [tile("stage%d" % a, PACK * H, BF16) for a in range(2)]
        w1_codes = [tile("codes%d" % a, H, U32) for a in range(2)]
        w1_sc = [tile("scales%d" % a, H, U8) for a in range(2)]

        def cast_w1(copy, a, b, first, count):
            dst = w1_stage[a][:, b * PACK * PASS:(b + 1) * PACK * PASS].rearrange("p (t m j) -> p m t j", t=PACK, j=PACK)
            src = w1_raw[a, b][:].rearrange("p (j m t) -> p m t j", j=PACK, t=PACK)
            copy(out=dst[:, :, first:first + count, :], in_=src[:, :, first:first + count, :])

        def quantize_w1(a, first, count):
            quantize(w1_codes[a], w1_sc[a], w1_stage[a], first * P, count * P)

        nc.vector.tensor_copy(v_words[0][:], table[0][:].bitcast(U32).indirect(idx[:]))
        nc.vector.tensor_copy(v_sc[:], table_sc[:].indirect(idx[:]))
        cast_w1(nc.scalar.copy, 0, 0, 0, PACK)
        quantize_w1(0, 0, PACK)
        cast_w1(nc.vector.tensor_copy, 1, 0, 0, PACK)
        quantize_w1(1, 0, PACK)
        v_words.append(tile("table_sc", S, U32))
        for c in range(2):
            nc.vector.tensor_copy(v_words[1][:, c * HALF:(c + 1) * HALF],
                                  table[1][:].bitcast(U32).indirect(idx[:, 32 * c:32 * (c + 1)]))

        cloth_sb = []
        wgt_sb = tile("wgt", PCOLS, F32)
        nc.sync.dma_start(out=wgt_sb[:], in_=wgt)

        def load_cloth(b):
            t = tile("big%d" % b, PACK * PCOLS, F32)
            nc.sync.dma_start(out=t[:].rearrange("p (j c) -> p j c", j=PACK), in_=rows_4p(cloth[b * PASS:(b + 1) * PASS, :]))
            cloth_sb.append(t)

        h = [tile("h%d" % b, PACK * S, F32) for b in range(2)]

        def h_cols(s, first, count):
            b, i = divmod(s, PACK)
            return h[b][:, i * S + first:i * S + first + count]

        def bounded(s, first, count, k):
            acc = bank(k % 4)
            cols = slice(first, first + count)
            for a in range(2):
                nc.tensor.matmul_mx(out=acc[:, 0:count], lhsT=w1_codes[a][:, s * P:(s + 1) * P].bitcast(FP8X4),
                                    lhsT_scale=w1_sc[a][:, s * P:(s + 1) * P], rhs=v_words[a][:, cols].bitcast(FP8X4),
                                    rhs_scale=v_sc[4 * a:P, cols], start=(a == 0), stop=(a == 1))
            nc.scalar.activation(out=h_cols(s, first, count), in_=acc[:, 0:count], func=ACT.Tanh)

        def file_h(s, first, count, on_vector=False):
            part = h_cols(s, first, count)
            if on_vector:
                nc.vector.tensor_scalar_mul(part, part, gain_sb[:, s:s + 1])
            else:
                nc.scalar.activation(out=part, in_=part, func=ACT.Copy, scale=gain_sb[:, s:s + 1])
            nc.vector.tensor_tensor(pages[s % PACK][:].indirect(idx2[:, first // 16:(first + count) // 16]), part,
                                    wgs_sb[:, first:first + count], ALU.mult)

        def make_h(s):
            for c in range(2):
                bounded(s, c * HALF, HALF, 2 * s + c + 1)
            file_h(s, 0, S)

        def interleave(dst, src, width, first, count):
            d = dst[:].rearrange("p (c i t) -> p c t i", i=PACK, t=PACK)
            r = src[:].rearrange("p (t c i) -> p c t i", t=PACK, i=PACK)
            nc.scalar.copy(out=d[:, first // PACK:(first + count) // PACK], in_=r[:, first // PACK:(first + count) // PACK])

        def quantize_weight(name, src, slots, stage_tag):
            staged = tile(stage_tag, 2 * PACK * N, BF16)
            for b in range(2):
                raw = load_rows(slots[b], src, b, slice(0, N))
                nc.scalar.copy(out=staged[:, b * PACK * N:(b + 1) * PACK * N].rearrange("p (c i t) -> p c t i", i=PACK, t=PACK),
                               in_=raw[:].rearrange("p (t c i) -> p c t i", t=PACK, i=PACK))
            codes = tile(name + "_codes", 2 * N, U32)
            scales = tile(name + "_sc", 2 * N, U8)
            quantize(codes, scales, staged, 0, 512)
            quantize(codes, scales, staged, 512, 256)
            return codes, scales

        h_codes = [tile("h_codes%d" % b, S, U32) for b in range(2)]
        h_sc = [tile("h_sc%d" % b, S, U8) for b in range(2)]

        def round_h(b):
            staged = tile("stage%d" % b, PACK * S, BF16)
            for c in range(2):
                interleave(staged, h[b], S, c * HALF, HALF)
            return staged

        def gather(x, i, first, count):
            nc.vector.tensor_tensor(x[:, i * PCOLS + first:i * PCOLS + first + count],
                                    pages[i][:].indirect(idx3[:, first // 16:(first + count) // 16]),
                                    wgt_sb[:, first:first + count], ALU.mult)

        def transpose_into(acc, src, i, jt, start, stop):
            nc.tensor.matmul(acc[:, i * P:(i + 1) * P], lhsT=src[:, i * PCOLS + jt * P:i * PCOLS + (jt + 1) * P],
                             rhs=ident[:], is_transpose=True, start=start, stop=stop)

        def open_sum(b, jt):
            acc = bank(jt % 4)
            for i in range(PACK):
                transpose_into(acc, cloth_sb[b], i, jt, i == 0, False)
            return acc

        def round_sum(acc, jt):
            turned = tile("turned%d" % (jt % 4), PASS, BF16)
            nc.scalar.copy(out=turned[:].rearrange("j (u p e) -> j u p e", u=2, e=2),
                           in_=acc[:].rearrange("j (u e p) -> j u p e", u=2, e=2))
            return turned

        def turn_back(staged, turned, jt, at):
            back = bank(4 + (jt // 2) % 2)
            count = len(turned)
            for t in range(count):
                words = turned[t][:].bitcast(F32)
                for u in range(2):
                    nc.tensor.transpose(back[:, (2 * t + u) * P:(2 * t + u + 1) * P], words[:, u * P:(u + 1) * P], ident[:])
            nc.scalar.copy(out=staged[:].bitcast(F32)[:, 2 * at * P:2 * (at + count) * P].rearrange("p (t j u) -> p t j u", t=count, u=2),
                           in_=back[:, 0:2 * count * P].rearrange("p (t u j) -> p t j u", t=count, u=2))

        bounded(0, 0, 256, 0)
        file_h(0, 0, 256, True)
        bounded(1, 0, HALF, 1)
        file_h(1, 0, HALF)
        bounded(0, 256, 256, 2)
        bounded(0, HALF, HALF, 3)
        file_h(0, 256, 768)
        bounded(1, HALF, HALF, 4)
        file_h(1, HALF, HALF)
        for a in range(2):
            cast_w1(nc.scalar.copy, a, 1, 0, PACK)
            quantize_w1(a, PACK, PACK)
            make_h(2 + a)
        load_cloth(0)
        x0 = tile("x0", PACK * PCOLS, F32)
        for i in range(PACK):
            gather(x0, i, 0, PCOLS)

        wc_codes, wc_sc = quantize_weight("wc", wc, (0, 1), "stage2")
        quantize(h_codes[0], h_sc[0], round_h(0), 0, S)
        wb_codes, wb_sc = quantize_weight("wb", wb, (0, 1), "stage3")
        for s in range(PACK, 2 * PACK):
            make_h(s)
        load_cloth(1)
        wa_codes = tile("wa_codes", 2 * 2 * N, U8)
        nc.sync.dma_start(out=wa_codes[:].rearrange("p (a n) -> p a n", a=2).bitcast(I32),
                          in_=wa_words.rearrange("a p n -> p a n").bitcast(I32))
        wa_sc = tile("wa_sc", 2 * N, U8)
        nc.vector.memset(wa_sc[:].bitcast(I32), 0)
        for q in range(4):
            nc.sync.dma_start(out=wa_sc[32 * q:32 * q + 4, :].rearrange("r (a n) -> r a n", a=2).bitcast(I32),
                              in_=wa_scales[:, 4 * q:4 * q + 4, :].rearrange("a r n -> r a n").bitcast(I32))
        cap_sb = tile("cap", N // P, F32)
        with nc.allow_non_contiguous_dma(reason="one value of cap for each partition"):
            nc.sync.dma_start(out=cap_sb[:], in_=cap.rearrange("(t p) -> p t", p=P))

        z_codes = [tile("codes%d" % b, PCOLS, U32) for b in range(2)]
        z_sc = [tile("scales%d" % b, PCOLS, U8) for b in range(2)]
        z0_stage = tile("stage2", PACK * PCOLS, BF16)
        z1_stage = [tile("stage%d" % (4 - c), PACK * HALF, BF16) for c in range(2)]
        for jp in range(0, PCOLS // P, 2):
            pair = []
            for jt in (jp, jp + 1):
                acc = open_sum(0, jt)
                for i in range(PACK):
                    transpose_into(acc, x0, i, jt, False, i == PACK - 1)
                pair.append(round_sum(acc, jt))
            turn_back(z0_stage, pair, jp, jp)
        quantize(z_codes[0], z_sc[0], z0_stage, 0, PCOLS)

        sums = [open_sum(1, jt) for jt in range(4)]
        h1_stage = round_h(1)
        yc = [tile("raw%d" % c, (N // P) * HALF, F32) for c in range(2)]

        def make_yc(c):
            for nt in range(N // P):
                acc = bank(6 + (3 * c + nt) % 2)
                for b in range(2):
                    w = slice(b * N + nt * P, b * N + (nt + 1) * P)
                    nc.tensor.matmul_mx(out=acc[:], lhsT=wc_codes[:, w].bitcast(FP8X4), lhsT_scale=wc_sc[:, w],
                                        rhs=h_codes[b][:, c * HALF:(c + 1) * HALF].bitcast(FP8X4),
                                        rhs_scale=h_sc[b][:, c * HALF:(c + 1) * HALF], start=(b == 0), stop=(b == 1))
                nc.scalar.activation(out=yc[c][:, nt * HALF:(nt + 1) * HALF], in_=acc[:], func=ACT.Identity,
                                     bias=cap_sb[:, nt:nt + 1])

        quantize(h_codes[1], h_sc[1], h1_stage, 0, HALF)
        make_yc(0)
        x1 = tile("h1", PACK * PCOLS, F32)
        for i in range(PACK):
            gather(x1, i, 0, HALF)
            for jt in range(4):
                transpose_into(sums[jt], x1, i, jt, False, i == PACK - 1)
        quantize(h_codes[1], h_sc[1], h1_stage, HALF, HALF)
        for jp in range(0, 4, 2):
            turn_back(z1_stage[0], [round_sum(sums[jt], jt) for jt in (jp, jp + 1)], jp, jp)
        make_yc(1)
        sums = {jt: open_sum(1, jt) for jt in range(4, 7)}
        for i in range(PACK):
            gather(x1, i, HALF, 3 * P)
            for jt in range(4, 7):
                transpose_into(sums[jt], x1, i, jt, False, i == PACK - 1)
        quantize(z_codes[1], z_sc[1], z1_stage[0], 0, HALF)
        x_last = tile("stage4", PACK * P, F32)
        for i in range(PACK):
            nc.vector.tensor_tensor(x_last[:, i * P:(i + 1) * P], pages[i][:].indirect(idx3[:, 7 * P // 16:]),
                                    wgt_sb[:, 7 * P:], ALU.mult)
        turn_back(z1_stage[1], [round_sum(sums[jt], jt) for jt in (4, 5)], 4, 0)
        turn_back(z1_stage[1], [round_sum(sums[6], 6)], 6, 2)

        nc.vector.tensor_tensor(z1_stage[1][:, 3 * PASS:].rearrange("p (c i t) -> p c t i", i=PACK, t=PACK),
                                x_last[:].rearrange("p (t c i) -> p c t i", t=PACK, i=PACK),
                                cloth_sb[1][:].rearrange("p (t c i) -> p c t i", t=PACK, i=PACK)[:, 7 * P // PACK:], ALU.add)

        scratch = tile("h0", PACK * PCOLS, F32)
        out_banks = ((6, 7), (3, 0), (6, 7), (1, 2), (4, 5), (3, 0))

        def finish(k, pieces):
            c, nt = divmod(k, N // P)
            width = HALF // pieces
            for first in range(0, HALF, width):
                result = yc[c][:, nt * HALF + first:nt * HALF + first + width]
                nc.vector.tensor_tensor(result, scratch[:, k * HALF + first:k * HALF + first + width], result, ALU.min)
                nc.sync.dma_start(out=out[nt * P:(nt + 1) * P, c * HALF + first:c * HALF + first + width], in_=result)

        for c in range(2):
            cols = slice(c * HALF, (c + 1) * HALF)
            if c == 1:
                nc.vector.quantize_mx(out=z_codes[1][:, HALF:].bitcast(FP8X4), scales=z_sc[1][:, HALF:], in_=z1_stage[1][:])
            for nt in range(N // P):
                k = 3 * c + nt
                ya = bank(out_banks[k][0])
                yb = bank(out_banks[k][1])
                for b in range(2):
                    w = slice(b * N + nt * P, b * N + (nt + 1) * P)
                    nc.tensor.matmul_mx(out=ya[:], lhsT=wa_codes[:, 2 * w.start:2 * w.stop].bitcast(FP4X4),
                                        lhsT_scale=wa_sc[:, w], rhs=z_codes[b][:, cols].bitcast(FP8X4),
                                        rhs_scale=z_sc[b][:, cols], start=(b == 0), stop=(b == 1))
                for b in range(2):
                    w = slice(b * N + nt * P, b * N + (nt + 1) * P)
                    nc.tensor.matmul_mx(out=yb[:], lhsT=wb_codes[:, w].bitcast(FP8X4), lhsT_scale=wb_sc[:, w],
                                        rhs=z_codes[b][:, cols].bitcast(FP8X4), rhs_scale=z_sc[b][:, cols],
                                        start=(b == 0), stop=(b == 1))
                larger = scratch[:, k * HALF:(k + 1) * HALF]
                nc.scalar.copy(out=larger, in_=ya[:])
                nc.vector.tensor_tensor(larger, larger, yb[:], ALU.max)
                if k > 0:
                    finish(k - 1, 1)
        finish(5, 2)
